import numpy as np
import ml_dtypes

BF16 = ml_dtypes.bfloat16


def bf(x):
    return np.asarray(x, np.float32).astype(BF16)


def f32(x):
    return np.asarray(x, np.float32)


def f64(x):
    return np.asarray(x).astype(np.float64)


def striped(idx):
    return np.tile(idx.reshape(-1, 16).T, (8, 1))


def rows(idx, k):
    return np.tile(idx, (k, 1))


def look(tab, idx):
    return np.take_along_axis(f64(tab), rows(idx, len(tab)), axis=1)


K, S, V, N, M = 256, 2048, 1024, 1024, 256


def setup_inputs():
    return {"tab": f32(np.random.standard_normal((K, S))), "w": bf(np.random.standard_normal((K, M)) / np.sqrt(K)), "offs": striped(np.random.randint(0, S, N))}


def reference(tab, w, offs):
    idx = offs[:16].T.reshape(-1)
    t = look(tab, idx)
    x = (t - 0.125) * 1.5
    y = f64(w).T @ x
    return y

@@ -1,0 +1,58 @@
+import concourse.mybir as mybir
+
+P = 128
+ROWS, TABLE, N, M = 256, 2048, 1024, 256
+PIECE = 512
+ROW_BLOCKS, OUT_BLOCKS, PIECES = ROWS // P, M // P, N // PIECE
+CENTRE, SCALE = 0.125, 1.5
+FLOPS = 2 * ROWS * M * N
+
+F32, BF16, U16 = mybir.dt.float32, mybir.dt.bfloat16, mybir.dt.uint16
+MULT, ADD = mybir.AluOpType.mult, mybir.AluOpType.add
+
+
+def tile_lookup_deq_nrm_none_kernel(tc, tab, w, offs, out):
+    nc = tc.nc
+    with (
+        tc.tile_pool(name="held", bufs=1) as held,
+        tc.psum_pool(name="psum", bufs=1) as psum,
+    ):
+        offsets = held.tile([P, N // 16], U16, name="offsets")
+        nc.sync.dma_start(offsets[:], offs)
+        windows = []
+        for r in range(ROW_BLOCKS):
+            window = held.tile([P, TABLE], F32, name=f"window{r}")
+            nc.sync.dma_start(window[:], tab[r * P : (r + 1) * P, :])
+            windows.append(window)
+        weights = []
+        for r in range(ROW_BLOCKS):
+            weight = held.tile([P, M], BF16, name=f"weight{r}")
+            nc.scalar.dma_start(weight[:], w[r * P : (r + 1) * P, :])
+            weights.append(weight)
+
+        banks = {}
+        for m in range(OUT_BLOCKS):
+            for n in range(PIECES):
+                banks[m, n] = psum.tile([P, PIECE], F32, name=f"bank{m}_{n}")
+
+        for r in range(ROW_BLOCKS):
+            for n in range(PIECES):
+                entries = offsets[:, n * (PIECE // 16) : (n + 1) * (PIECE // 16)]
+                x = held.tile([P, PIECE], BF16, name=f"x{r}_{n}")
+                nc.vector.tensor_scalar(
+                    x[:], windows[r][:].indirect(entries), SCALE, -CENTRE * SCALE, MULT, ADD
+                )
+                for m in range(OUT_BLOCKS):
+                    nc.tensor.matmul(
+                        banks[m, n][:],
+                        weights[r][:, m * P : (m + 1) * P],
+                        x[:],
+                        start=(r == 0),
+                        stop=(r == ROW_BLOCKS - 1),
+                    )
+
+        for n in range(PIECES):
+            for m in range(OUT_BLOCKS):
+                staged = held.tile([P, PIECE], F32, name=f"staged{m}_{n}")
+                nc.scalar.copy(staged[:], banks[m, n][:])
+                nc.sync.dma_start(out[m * P : (m + 1) * P, n * PIECE : (n + 1) * PIECE], staged[:])

@@ -2,7 +2,7 @@ import concourse.mybir as mybir
 
 P = 128
 ROWS, TABLE, N, M = 256, 2048, 1024, 256
-PIECE = 512
+PIECE = 256
 ROW_BLOCKS, OUT_BLOCKS, PIECES = ROWS // P, M // P, N // PIECE
 CENTRE, SCALE = 0.125, 1.5
 FLOPS = 2 * ROWS * M * N
@@ -19,16 +19,12 @@ def tile_lookup_deq_nrm_none_kernel(tc, tab, w, offs, out):
     ):
         offsets = held.tile([P, N // 16], U16, name="offsets")
         nc.sync.dma_start(offsets[:], offs)
-        windows = []
-        for r in range(ROW_BLOCKS):
-            window = held.tile([P, TABLE], F32, name=f"window{r}")
-            nc.sync.dma_start(window[:], tab[r * P : (r + 1) * P, :])
-            windows.append(window)
-        weights = []
-        for r in range(ROW_BLOCKS):
-            weight = held.tile([P, M], BF16, name=f"weight{r}")
-            nc.scalar.dma_start(weight[:], w[r * P : (r + 1) * P, :])
-            weights.append(weight)
+        windows = [held.tile([P, TABLE], F32, name=f"window{r}") for r in range(ROW_BLOCKS)]
+        weights = held.tile([P, ROW_BLOCKS, M], BF16, name="weights")
+        nc.sync.dma_start(windows[0][:], tab[0:P, :])
+        nc.sync.dma_start(weights[:], w.rearrange("(r p) m -> p r m", p=P))
+        for r in range(1, ROW_BLOCKS):
+            nc.sync.dma_start(windows[r][:], tab[r * P : (r + 1) * P, :])
 
         banks = {}
         for m in range(OUT_BLOCKS):
@@ -37,6 +33,7 @@ def tile_lookup_deq_nrm_none_kernel(tc, tab, w, offs, out):
 
         for r in range(ROW_BLOCKS):
             for n in range(PIECES):
+                columns = slice(n * PIECE, (n + 1) * PIECE)
                 entries = offsets[:, n * (PIECE // 16) : (n + 1) * (PIECE // 16)]
                 x = held.tile([P, PIECE], BF16, name=f"x{r}_{n}")
                 nc.vector.tensor_scalar(
@@ -45,14 +42,17 @@ def tile_lookup_deq_nrm_none_kernel(tc, tab, w, offs, out):
                 for m in range(OUT_BLOCKS):
                     nc.tensor.matmul(
                         banks[m, n][:],
-                        weights[r][:, m * P : (m + 1) * P],
+                        weights[:, r, m * P : (m + 1) * P],
                         x[:],
                         start=(r == 0),
                         stop=(r == ROW_BLOCKS - 1),
                     )
-
-        for n in range(PIECES):
-            for m in range(OUT_BLOCKS):
-                staged = held.tile([P, PIECE], F32, name=f"staged{m}_{n}")
-                nc.scalar.copy(staged[:], banks[m, n][:])
-                nc.sync.dma_start(out[m * P : (m + 1) * P, n * PIECE : (n + 1) * PIECE], staged[:])
+                if r < ROW_BLOCKS - 1:
+                    continue
+                staged = held.tile([P, OUT_BLOCKS, PIECE], F32, name=f"staged{n}")
+                for m in range(OUT_BLOCKS):
+                    if n == PIECES - 1 and m == OUT_BLOCKS - 1:
+                        nc.vector.tensor_copy(staged[:, m, :], banks[m, n][:])
+                    else:
+                        nc.scalar.copy(staged[:, m, :], banks[m, n][:])
+                nc.sync.dma_start(out.rearrange("(m p) n -> p m n", p=P)[:, :, columns], staged[:])

@@ -18,10 +18,10 @@ def tile_lookup_deq_nrm_none_kernel(tc, tab, w, offs, out):
         tc.psum_pool(name="psum", bufs=1) as psum,
     ):
         offsets = held.tile([P, N // 16], U16, name="offsets")
-        nc.sync.dma_start(offsets[:], offs)
         windows = [held.tile([P, TABLE], F32, name=f"window{r}") for r in range(ROW_BLOCKS)]
         weights = held.tile([P, ROW_BLOCKS, M], BF16, name="weights")
         nc.sync.dma_start(windows[0][:], tab[0:P, :])
+        nc.sync.dma_start(offsets[:], offs)
         nc.sync.dma_start(weights[:], w.rearrange("(r p) m -> p r m", p=P))
         for r in range(1, ROW_BLOCKS):
             nc.sync.dma_start(windows[r][:], tab[r * P : (r + 1) * P, :])

import concourse.mybir as mybir

P = 128
ROWS, TABLE, N, M = 256, 2048, 1024, 256
PIECE = 256
ROW_BLOCKS, OUT_BLOCKS, PIECES = ROWS // P, M // P, N // PIECE
CENTRE, SCALE = 0.125, 1.5
FLOPS = 2 * ROWS * M * N

F32, BF16, U16 = mybir.dt.float32, mybir.dt.bfloat16, mybir.dt.uint16
MULT, ADD = mybir.AluOpType.mult, mybir.AluOpType.add


def tile_lookup_deq_nrm_none_kernel(tc, tab, w, offs, out):
    nc = tc.nc
    with (
        tc.tile_pool(name="held", bufs=1) as held,
        tc.psum_pool(name="psum", bufs=1) as psum,
    ):
        offsets = held.tile([P, N // 16], U16, name="offsets")
        windows = [held.tile([P, TABLE], F32, name=f"window{r}") for r in range(ROW_BLOCKS)]
        weights = held.tile([P, ROW_BLOCKS, M], BF16, name="weights")
        nc.sync.dma_start(windows[0][:], tab[0:P, :])
        nc.sync.dma_start(offsets[:], offs)
        nc.sync.dma_start(weights[:], w.rearrange("(r p) m -> p r m", p=P))
        for r in range(1, ROW_BLOCKS):
            nc.sync.dma_start(windows[r][:], tab[r * P : (r + 1) * P, :])

        banks = {}
        for m in range(OUT_BLOCKS):
            for n in range(PIECES):
                banks[m, n] = psum.tile([P, PIECE], F32, name=f"bank{m}_{n}")

        for r in range(ROW_BLOCKS):
            for n in range(PIECES):
                columns = slice(n * PIECE, (n + 1) * PIECE)
                entries = offsets[:, n * (PIECE // 16) : (n + 1) * (PIECE // 16)]
                x = held.tile([P, PIECE], BF16, name=f"x{r}_{n}")
                nc.vector.tensor_scalar(
                    x[:], windows[r][:].indirect(entries), SCALE, -CENTRE * SCALE, MULT, ADD
                )
                for m in range(OUT_BLOCKS):
                    nc.tensor.matmul(
                        banks[m, n][:],
                        weights[:, r, m * P : (m + 1) * P],
                        x[:],
                        start=(r == 0),
                        stop=(r == ROW_BLOCKS - 1),
                    )
                if r < ROW_BLOCKS - 1:
                    continue
                staged = held.tile([P, OUT_BLOCKS, PIECE], F32, name=f"staged{n}")
                for m in range(OUT_BLOCKS):
                    if n == PIECES - 1 and m == OUT_BLOCKS - 1:
                        nc.vector.tensor_copy(staged[:, m, :], banks[m, n][:])
                    else:
                        nc.scalar.copy(staged[:, m, :], banks[m, n][:])
                nc.sync.dma_start(out.rearrange("(m p) n -> p m n", p=P)[:, :, columns], staged[:])
